import numpy as np
import ml_dtypes


def mxq(x, axis, fmt="e4m3"):
    dtype, down = {"e4m3": (ml_dtypes.float8_e4m3fn, 7), "e5m2": (ml_dtypes.float8_e5m2, 14)}[fmt]
    v = np.moveaxis(np.asarray(x, np.float32).astype(ml_dtypes.bfloat16).astype(np.float64), axis, -1)
    blocks = v.reshape(v.shape[:-1] + (-1, 32))
    amax = np.abs(blocks).max(-1, keepdims=True)
    byte = np.maximum(np.where(amax > 0, np.frexp(amax)[1] - 1 + 127, 0) - down, 1)
    scale = np.exp2(byte - 127.0)
    codes = (blocks / scale).astype(np.float32).astype(dtype).astype(np.float64)
    return np.moveaxis((codes * scale).reshape(v.shape), -1, axis)


WIDE = False


def mx_kscale(k):
    if not WIDE:
        return np.ones(k)
    levels = np.array([10, -10, 5, -5, 0])
    if k % 512:
        return np.exp2(np.random.permutation(np.resize(levels, k // 32))).repeat(32)
    a = np.empty((k // 512, 16))
    for p in range(k // 512):
        a[p, :8] = np.random.permutation(np.resize(levels, 8))
        for g in range(8):
            far = levels[np.abs(levels - a[p, g]) >= 10]
            a[p, g + 8] = far[np.random.randint(len(far))]
    return np.exp2(a.ravel()).repeat(32)


def f64(x):
    return np.asarray(x).astype(np.float64)


def striped(idx):
    return np.tile(idx.reshape(-1, 16).T, (8, 1)).astype(np.uint16)


def unstriped(offs):
    return offs[:16].T.reshape(-1).astype(np.int64)


E2M1 = np.array([0.0, 0.5, 1.0, 1.5, 2.0, 3.0, 4.0, 6.0, -0.0, -0.5, -1.0, -1.5, -2.0, -3.0, -4.0, -6.0])


def pack_weight(w, fmt):
    k, n = w.shape
    w = f64(np.asarray(w, np.float32).astype(ml_dtypes.bfloat16)).reshape(k // 32, 32, n)
    amax = np.abs(w).max(1)
    if fmt == "e4m3":
        byte = np.frexp(amax)[1] - 1 + 127 - 7
    else:
        mant, ex = np.frexp(amax / 6.0)
        byte = np.where(mant > 0.5, ex, ex - 1) + 127
    byte = np.clip(np.where(amax > 0, byte, 1), 1, 254)
    scaled = (w * np.exp2(127.0 - byte)[:, None, :]).reshape(k, n).astype(np.float32)
    by_word = np.ascontiguousarray(scaled.reshape(k // 512, 128, 4, n).transpose(0, 1, 3, 2))
    if fmt == "e4m3":
        words = by_word.astype(ml_dtypes.float8_e4m3fn).view(np.uint8)
    else:
        c = by_word.astype(ml_dtypes.float4_e2m1fn).view(np.uint8) & 0xF
        words = (c[..., 0::2] | (c[..., 1::2] << 4)).reshape(k // 512, 128, 2 * n)
    return np.ascontiguousarray(words), np.ascontiguousarray(byte.astype(np.uint8).reshape(k // 512, 16, n))


def unpack_weight(words, scales, fmt):
    g, _, n = scales.shape
    words = np.ascontiguousarray(words).reshape(g, 128, n, -1)
    if fmt == "e4m3":
        vals = words.view(ml_dtypes.float8_e4m3fn).astype(np.float64)
    else:
        nib = np.empty((g, 128, n, 4), np.uint8)
        nib[..., 0::2] = words & 0xF
        nib[..., 1::2] = words >> 4
        vals = E2M1[nib]
    vals = vals * np.repeat(np.exp2(scales.astype(np.float64) - 127.0), 8, axis=1)[..., None]
    return vals.transpose(0, 1, 3, 2).reshape(g * 512, n)


def gelu(v):
    return 0.5 * v * (1.0 + np.tanh(np.sqrt(2.0 / np.pi) * (v + 0.044715 * v**3)))


K, T, S, T2, P, H, N = 512, 2048, 1024, 2048, 512, 1024, 384

def setup_inputs():
    n = np.random.standard_normal
    s = mx_kscale(K)[:, None]
    u = mx_kscale(H)[:, None]
    tab_words, tab_scales = pack_weight(n((K, T)) * s, "e4m3")
    w2_words, w2_scales = pack_weight(n((K, H)) / np.sqrt(K) / s, "e2m1")
    perm = np.random.permutation(T2)
    return {
        "tab_words": tab_words, "tab_scales": tab_scales,
        "offs": striped(np.random.permutation(T)[:S]),
        "w1": (n((K, H)) / np.sqrt(K) / s).astype(np.float32),
        "b1": (0.7 * n(H)).astype(np.float32),
        "w2_words": w2_words, "w2_scales": w2_scales,
        "gain": (np.exp(0.3 * n(H)) * u[:, 0]).astype(np.float32),
        "wgs": np.exp(0.3 * n((128, S))).astype(np.float32),
        "page0": (n((H, T2)) * u).astype(np.float32),
        "offs2": striped(np.random.permutation(T2)[:S]),
        "offs3": striped(perm[:P]),
        "offs4": striped(perm[P:2 * P]),
        "d": (n((H, P)) * u).astype(np.float32),
        "w3": (n((H, N)) / np.sqrt(H) / u).astype(np.float32),
    }

def reference(tab_words, tab_scales, offs, w1, b1, w2_words, w2_scales, gain, wgs, page0, offs2, offs3, offs4, d, w3):
    v = unpack_weight(tab_words, tab_scales, "e4m3")[:, unstriped(offs)]
    w2 = unpack_weight(w2_words, w2_scales, "e2m1")
    y1 = (mxq(f64(w1), 0, "e4m3").T @ v) + f64(b1)[:, None]
    y2 = w2.T @ v
    h = f64(gain)[:, None] * np.minimum(y1, y2)
    page = f64(page0).copy()
    page[:, unstriped(offs2)] = np.tile(f64(wgs), (H // 128, 1)) * h
    a = page[:, unstriped(offs3)]
    b = page[:, unstriped(offs4)]
    page[:, unstriped(offs3)] = a + b + f64(d)
    page[:, unstriped(offs4)] = np.maximum(a, b)
    y = mxq(f64(w3), 0, "e4m3").T @ mxq(page, 0, "e4m3")
    out = 0.5 * y * (1.0 + np.tanh(np.sqrt(2.0 / np.pi) * (y + 0.044715 * y ** 3)))
    return out

@@ -1,0 +1,283 @@
+from contextlib import ExitStack
+
+import concourse.mybir as mybir
+
+K, T, S, T2, PAIRS, H, N = 512, 2048, 1024, 2048, 512, 1024, 384
+FLOPS = 2 * 2 * K * H * S + 2 * H * N * T2
+
+F32 = mybir.dt.float32
+BF16 = mybir.dt.bfloat16
+I32 = mybir.dt.int32
+U32 = mybir.dt.uint32
+U16 = mybir.dt.uint16
+U8 = mybir.dt.uint8
+FP8X4 = mybir.dt.float8_e4m3fn_x4
+FP4X4 = mybir.dt.float4_e2m1fn_x4
+ALU = mybir.AluOpType
+ACT = mybir.ActivationFunctionType
+
+P = 128
+PACK = 4
+BANK = 512
+PASSES = H // (P * PACK)
+SLICES = PASSES * PACK
+HALVES = S // BANK
+CHUNKS = T2 // BANK
+N_TILES = N // P
+BANKS = 8
+
+
+def tile_list_wine_lot_sequencing_kernel(
+    tc, tab_words, tab_scales, offs, w1, b1, w2_words, w2_scales, gain, wgs, page0, offs2, offs3, offs4, d, w3, out
+):
+    nc = tc.nc
+    with ExitStack() as ctx:
+        lists = ctx.enter_context(tc.tile_pool(name="lists", bufs=1))
+        keep = ctx.enter_context(tc.tile_pool(name="keep", bufs=1))
+        two = ctx.enter_context(tc.tile_pool(name="two", bufs=2))
+        three = ctx.enter_context(tc.tile_pool(name="three", bufs=3))
+        four = ctx.enter_context(tc.tile_pool(name="four", bufs=4))
+        psum = ctx.enter_context(tc.psum_pool(name="psum", bufs=BANKS))
+
+        def load_list(name, src):
+            tile = lists.tile(list(src.shape), U16, name=name)
+            nc.sync.dma_start(tile[:], src)
+            return tile
+
+        def load_scale_rows(name, src, width, engine):
+            tile = keep.tile([P, width], U8, name=name, align_bytes=64)
+            engine.memset(tile[:].bitcast(I32), 0)
+            for q in range(4):
+                nc.sync.dma_start(tile[32 * q : 32 * q + 4, :].bitcast(I32), src[0, 4 * q : 4 * q + 4, :].bitcast(I32))
+            return tile
+
+        idx = load_list("idx", offs)
+        table_scales = load_scale_rows("table_scales", tab_scales, T, nc.vector)
+        table_words = keep.tile([P, T], U32, align_bytes=64)
+        nc.sync.dma_start(table_words[:].bitcast(I32), tab_words[0].rearrange("p t i -> p (t i)").bitcast(I32))
+
+        w1_rows = w1.rearrange("(p j) (b c) -> b p j c", j=PACK, b=PASSES)
+        w1_raw = {}
+
+        def load_w1(b):
+            w1_raw[b] = keep.tile([P, PACK, P * PACK], F32, name=f"w1_raw{b}")
+            nc.sync.dma_start(w1_raw[b][:], w1_rows[b])
+
+        load_w1(0)
+        w2_raw = keep.tile([P, H], U16, align_bytes=64)
+        nc.sync.dma_start(w2_raw[:].bitcast(I32), w2_words[0].bitcast(I32))
+        w2_raw_scales = load_scale_rows("w2_raw_scales", w2_scales, H, nc.gpsimd)
+        b1_cols = keep.tile([P, PASSES, PACK], F32)
+        nc.sync.dma_start(b1_cols[:], b1.rearrange("(b p t) -> p b t", b=PASSES, t=PACK))
+        gain_cols = keep.tile([P, PASSES, PACK], F32)
+        nc.sync.dma_start(gain_cols[:], gain.rearrange("(b p t) -> p b t", b=PASSES, t=PACK))
+
+        wgs_rows = wgs.rearrange("(p t) j -> p t j", t=PACK)
+        wgs_first = keep.tile([P, 1, S], F32)
+        wgs_rest = keep.tile([P, PACK - 1, S], F32)
+        for q in range(4):
+            nc.sync.dma_start(wgs_first[32 * q : 32 * q + 32], wgs_rows[:, 0:1, :])
+        idx2 = load_list("idx2", offs2)
+
+        page_rows = page0.rearrange("(b p t) c -> b t p c", b=PASSES, t=PACK)
+        d_rows = d.rearrange("(b p t) m -> b t p m", b=PASSES, t=PACK)
+        pages, d_tiles = {}, {}
+
+        def load_slice(s):
+            b, t = divmod(s, PACK)
+            pages[s] = four.tile([P, T2], F32, name="page")
+            nc.sync.dma_start(pages[s][:], page_rows[b, t])
+            d_tiles[s] = four.tile([P, PAIRS], F32, name="d_tile")
+            nc.sync.dma_start(d_tiles[s][:], d_rows[b, t])
+
+        load_slice(0)
+        idx3 = load_list("idx3", offs3)
+        idx4 = load_list("idx4", offs4)
+        for q in range(4):
+            nc.sync.dma_start(wgs_rest[32 * q : 32 * q + 32], wgs_rows[:, 1:PACK, :])
+        load_slice(1)
+        load_w1(1)
+        load_slice(2)
+        w3_raw = keep.tile([P, PASSES, PACK, N], F32)
+        nc.sync.dma_start(w3_raw[:], w3.rearrange("(b p t) n -> p b t n", b=PASSES, t=PACK))
+        load_slice(3)
+
+        w2_codes = keep.tile([P, H], U16, align_bytes=64)
+        nc.scalar.copy(
+            w2_codes[:].rearrange("p (b t m) -> p b t m", b=PASSES, t=PACK),
+            w2_raw[:].rearrange("p (b m t) -> p b t m", b=PASSES, t=PACK),
+        )
+        w2_sc = keep.tile([P, H], U8, align_bytes=64)
+        nc.gpsimd.tensor_copy(
+            w2_sc[:].rearrange("p (b t m) -> p b t m", b=PASSES, t=PACK),
+            w2_raw_scales[:].rearrange("p (b m t) -> p b t m", b=PASSES, t=PACK),
+        )
+
+        v_words, v_scales = {}, {}
+
+        def gather_table(u):
+            part = idx[:, u * (BANK // 16) : (u + 1) * (BANK // 16)]
+            v_scales[u] = keep.tile([P, BANK], U8, name=f"v_scales{u}", align_bytes=64)
+            nc.vector.tensor_copy(v_scales[u][:], table_scales[:].indirect(part))
+            v_words[u] = keep.tile([P, BANK], U32, name=f"v_words{u}", align_bytes=64)
+            nc.vector.tensor_copy(v_words[u][:], table_words[:].indirect(part))
+
+        w1_codes, w1_sc = {}, {}
+
+        def quantize_w1(s):
+            b, t = divmod(s, PACK)
+            grouped = two.tile([P, P, PACK], BF16, name="w1_grouped", align_bytes=64)
+            nc.scalar.copy(grouped[:], w1_raw[b][:].rearrange("p j (m t) -> p t m j", t=PACK)[:, t])
+            w1_codes[s] = keep.tile([P, P], U32, name=f"w1_codes{s}", align_bytes=64)
+            w1_sc[s] = keep.tile([P, P], U8, name=f"w1_sc{s}", align_bytes=64)
+            nc.vector.quantize_mx(
+                out=w1_codes[s][:].bitcast(FP8X4), scales=w1_sc[s][:], in_=grouped[:].rearrange("p m j -> p (m j)")
+            )
+
+        factor, y1_banks, y2_tiles, h_tiles = {}, {}, {}, {}
+
+        def products(s):
+            b, t = divmod(s, PACK)
+            factor[s] = two.tile([P, S], F32, name="factor")
+            src = wgs_first[:, 0, :] if t == 0 else wgs_rest[:, t - 1, :]
+            nc.scalar.activation(factor[s][:], src, ACT.Copy, scale=gain_cols[:, b, t : t + 1])
+            y2_tiles[s] = three.tile([P, S], F32, name="y2")
+            cols = slice(s * P, (s + 1) * P)
+            for u in range(HALVES):
+                y2_bank = psum.tile([P, BANK], F32, name="bank")
+                nc.tensor.matmul_mx(
+                    out=y2_bank[:], lhsT=w2_codes[:, cols].bitcast(FP4X4), lhsT_scale=w2_sc[:, cols],
+                    rhs=v_words[u][:].bitcast(FP8X4), rhs_scale=v_scales[u][:], start=True, stop=True,
+                )
+                y1_banks[s, u] = psum.tile([P, BANK], F32, name="bank")
+                nc.tensor.matmul_mx(
+                    out=y1_banks[s, u][:], lhsT=w1_codes[s][:].bitcast(FP8X4), lhsT_scale=w1_sc[s][:],
+                    rhs=v_words[u][:].bitcast(FP8X4), rhs_scale=v_scales[u][:], start=True, stop=True,
+                )
+                nc.scalar.copy(y2_tiles[s][:, u * BANK : (u + 1) * BANK], y2_bank[:])
+
+        def lower_reading(s, u):
+            b, t = divmod(s, PACK)
+            if u == 0:
+                h_tiles[s] = two.tile([P, S], F32, name="h")
+            cols = slice(u * BANK, (u + 1) * BANK)
+            nc.vector.scalar_tensor_tensor(
+                out=h_tiles[s][:, cols], in0=y1_banks[s, u][:], scalar=b1_cols[:, b, t : t + 1],
+                in1=y2_tiles[s][:, cols], op0=ALU.add, op1=ALU.min,
+            )
+
+        def put_h(s, first, last):
+            cols = slice(first * BANK, last * BANK)
+            part = idx2[:, first * (BANK // 16) : last * (BANK // 16)]
+            nc.vector.tensor_tensor(pages[s][:].indirect(part), h_tiles[s][:, cols], factor[s][:, cols], ALU.mult)
+
+        firsts, seconds = {}, {}
+
+        def fetch_pairs(s):
+            firsts[s] = two.tile([P, PAIRS], F32, name="firsts")
+            nc.vector.tensor_copy(firsts[s][:], pages[s][:].indirect(idx3[:]))
+            seconds[s] = two.tile([P, PAIRS], F32, name="seconds")
+            nc.vector.tensor_copy(seconds[s][:], pages[s][:].indirect(idx4[:]))
+
+        grouped_page, page_codes, page_sc, last_two = {}, {}, {}, {}
+
+        def round_slice(s, c, copy):
+            b, t = divmod(s, PACK)
+            if t == 0:
+                grouped_page[b, c] = two.tile([P, BANK, PACK], BF16, name=f"grouped_page{c}", align_bytes=64)
+            copy(grouped_page[b, c][:, :, t], pages[s][:, c * BANK : (c + 1) * BANK])
+
+        def quantize_page(b, c):
+            page_codes[b, c] = keep.tile([P, BANK], U32, name=f"page_codes{b}{c}", align_bytes=64)
+            page_sc[b, c] = keep.tile([P, BANK], U8, name=f"page_sc{b}{c}", align_bytes=64)
+            nc.vector.quantize_mx(
+                out=page_codes[b, c][:].bitcast(FP8X4), scales=page_sc[b, c][:],
+                in_=grouped_page[b, c][:].rearrange("p m t -> p (m t)"),
+            )
+
+        w3_codes = keep.tile([P, PASSES, N], U32, align_bytes=64)
+        w3_sc = keep.tile([P, PASSES, N], U8, align_bytes=64)
+
+        def quantize_w3(b):
+            grouped = two.tile([P, N, PACK], BF16, name="w3_grouped", align_bytes=64)
+            nc.scalar.copy(grouped[:], w3_raw[:, b].rearrange("p t n -> p n t"))
+            nc.vector.quantize_mx(
+                out=w3_codes[:, b, :].bitcast(FP8X4), scales=w3_sc[:, b, :], in_=grouped[:].rearrange("p n t -> p (n t)")
+            )
+
+        gather_table(0)
+        quantize_w1(0)
+        gather_table(1)
+        products(0)
+        quantize_w1(1)
+        products(1)
+        for u in range(HALVES):
+            lower_reading(0, u)
+            put_h(0, u, u + 1)
+        for s in range(2, SLICES):
+            quantize_w1(s)
+
+        for s in range(SLICES):
+            if s + 2 < SLICES:
+                products(s + 2)
+            if s + 1 < SLICES:
+                for u in range(HALVES):
+                    lower_reading(s + 1, u)
+                work = y2_tiles[s + 1]
+            else:
+                work = three.tile([P, S], F32, name="y2")
+            if s == 0:
+                fetch_pairs(0)
+            first_plus_d, larger = work[:, 0:PAIRS], work[:, PAIRS : 2 * PAIRS]
+            nc.vector.tensor_tensor(first_plus_d, firsts[s][:], d_tiles[s][:], ALU.add)
+            nc.vector.tensor_tensor(larger, firsts[s][:], seconds[s][:], ALU.max)
+            if s + 1 < SLICES:
+                put_h(s + 1, 0, HALVES)
+            nc.vector.tensor_tensor(pages[s][:].indirect(idx3[:]), first_plus_d, seconds[s][:], ALU.add)
+            if s + 1 < SLICES:
+                fetch_pairs(s + 1)
+            nc.vector.tensor_copy(pages[s][:].indirect(idx4[:]), larger)
+            if s + 2 < SLICES:
+                for c in range(CHUNKS):
+                    round_slice(s, c, nc.scalar.copy)
+            if s + 2 == SLICES:
+                for c in range(CHUNKS):
+                    last_two[c] = keep.tile([P, 2, BANK], BF16, name=f"last_two{c}")
+                    nc.scalar.copy(last_two[c][:, 0, :], pages[s][:, c * BANK : (c + 1) * BANK])
+            if s < PASSES:
+                quantize_w3(s)
+            if s == PACK - 1:
+                for c in range(CHUNKS):
+                    quantize_page(0, c)
+            if s + 4 < SLICES:
+                load_slice(s + 4)
+
+        groups = [(c, n) for c in range(CHUNKS) for n in range(N_TILES)]
+        acc = {}
+
+        def second_stage_pass(c, n, b):
+            if b == 0:
+                acc[c, n] = psum.tile([P, BANK], F32, name="bank")
+            cols = slice(n * P, (n + 1) * P)
+            nc.tensor.matmul_mx(
+                out=acc[c, n][:], lhsT=w3_codes[:, b, cols].bitcast(FP8X4), lhsT_scale=w3_sc[:, b, cols],
+                rhs=page_codes[b, c][:].bitcast(FP8X4), rhs_scale=page_sc[b, c][:], start=(b == 0), stop=(b == PASSES - 1),
+            )
+
+        for c, n in groups[:BANKS]:
+            second_stage_pass(c, n, 0)
+        for step in range(CHUNKS + 2):
+            if step < CHUNKS:
+                nc.vector.tensor_copy(last_two[step][:, 1, :], pages[SLICES - 1][:, step * BANK : (step + 1) * BANK])
+            if 0 <= step - 1 < CHUNKS:
+                c = step - 1
+                nc.vector.tensor_copy(grouped_page[1, c][:, :, 2:PACK], last_two[c][:].rearrange("p e m -> p m e"))
+            if 0 <= step - 2:
+                quantize_page(1, step - 2)
+        for g, (c, n) in enumerate(groups):
+            if g >= BANKS:
+                second_stage_pass(c, n, 0)
+            second_stage_pass(c, n, 1)
+            result = four.tile([P, BANK], F32, name="result")
+            nc.scalar.activation(result[:], acc[c, n][:], ACT.Gelu_apprx_tanh)
+            nc.sync.dma_start(out[n * P : (n + 1) * P, c * BANK : (c + 1) * BANK], result[:])

@@ -1,6 +1,7 @@
 from contextlib import ExitStack
 
 import concourse.mybir as mybir
+from concourse.masks import make_identity
 
 K, T, S, T2, PAIRS, H, N = 512, 2048, 1024, 2048, 512, 1024, 384
 FLOPS = 2 * 2 * K * H * S + 2 * H * N * T2
@@ -25,6 +26,7 @@ HALVES = S // BANK
 CHUNKS = T2 // BANK
 N_TILES = N // P
 BANKS = 8
+PAGE_BUFS = 5
 
 
 def tile_list_wine_lot_sequencing_kernel(
@@ -35,24 +37,31 @@ def tile_list_wine_lot_sequencing_kernel(
         lists = ctx.enter_context(tc.tile_pool(name="lists", bufs=1))
         keep = ctx.enter_context(tc.tile_pool(name="keep", bufs=1))
         two = ctx.enter_context(tc.tile_pool(name="two", bufs=2))
-        three = ctx.enter_context(tc.tile_pool(name="three", bufs=3))
         four = ctx.enter_context(tc.tile_pool(name="four", bufs=4))
-        psum = ctx.enter_context(tc.psum_pool(name="psum", bufs=BANKS))
+        psum = ctx.enter_context(tc.psum_pool(name="psum", bufs=2))
+        bank_bufs = {"y1": HALVES, "y2": HALVES, "turn": 2, "spare": 2}
+
+        def new_bank(tag):
+            return psum.tile([P, BANK], F32, name="bank", tag=tag, bufs=bank_bufs[tag])
+
 
         def load_list(name, src):
             tile = lists.tile(list(src.shape), U16, name=name)
             nc.sync.dma_start(tile[:], src)
             return tile
 
-        def load_scale_rows(name, src, width, engine):
-            tile = keep.tile([P, width], U8, name=name, align_bytes=64)
-            engine.memset(tile[:].bitcast(I32), 0)
+        def load_scale_rows(queue, tile, src):
             for q in range(4):
-                nc.sync.dma_start(tile[32 * q : 32 * q + 4, :].bitcast(I32), src[0, 4 * q : 4 * q + 4, :].bitcast(I32))
-            return tile
+                queue.dma_start(tile[32 * q : 32 * q + 4, :].bitcast(I32), src[0, 4 * q : 4 * q + 4, :].bitcast(I32))
 
         idx = load_list("idx", offs)
-        table_scales = load_scale_rows("table_scales", tab_scales, T, nc.vector)
+        table_rows = keep.tile([P, T], U8)
+        load_scale_rows(nc.sync, table_rows, tab_scales)
+        table_scales = keep.tile([P, T], U8, align_bytes=64)
+        nc.vector.memset(table_scales[:].bitcast(I32), 0)
+        for q in range(4):
+            rows = slice(32 * q, 32 * q + 4)
+            nc.vector.tensor_copy(table_scales[rows, :].bitcast(I32), table_rows[rows, :].bitcast(I32))
         table_words = keep.tile([P, T], U32, align_bytes=64)
         nc.sync.dma_start(table_words[:].bitcast(I32), tab_words[0].rearrange("p t i -> p (t i)").bitcast(I32))
 
@@ -63,21 +72,41 @@ def tile_list_wine_lot_sequencing_kernel(
             w1_raw[b] = keep.tile([P, PACK, P * PACK], F32, name=f"w1_raw{b}")
             nc.sync.dma_start(w1_raw[b][:], w1_rows[b])
 
+        w2_rows = keep.tile([P, H], U8)
+        load_scale_rows(nc.sync, w2_rows, w2_scales)
+        w2_raw = {}
+
+        def load_w2(b):
+            w2_raw[b] = keep.tile([P, P * PACK], U16, name=f"w2_raw{b}")
+            nc.sync.dma_start(w2_raw[b][:].bitcast(I32), w2_words[0, :, 2 * b * P * PACK : 2 * (b + 1) * P * PACK].bitcast(I32))
+
         load_w1(0)
-        w2_raw = keep.tile([P, H], U16, align_bytes=64)
-        nc.sync.dma_start(w2_raw[:].bitcast(I32), w2_words[0].bitcast(I32))
-        w2_raw_scales = load_scale_rows("w2_raw_scales", w2_scales, H, nc.gpsimd)
-        b1_cols = keep.tile([P, PASSES, PACK], F32)
-        nc.sync.dma_start(b1_cols[:], b1.rearrange("(b p t) -> p b t", b=PASSES, t=PACK))
+        load_w2(0)
+        w2_raw_scales = keep.tile([P, H], U8, align_bytes=64)
+        nc.gpsimd.memset(w2_raw_scales[:].bitcast(I32), 0)
+        for q in range(4):
+            rows = slice(32 * q, 32 * q + 4)
+            nc.gpsimd.tensor_copy(w2_raw_scales[rows, :].bitcast(I32), w2_rows[rows, :].bitcast(I32))
+        b1_rows = b1.rearrange("(b p t o) -> b t p o", b=PASSES, t=PACK, o=1)
+        b1_cols = {}
+
+        def load_b1(s):
+            b, t = divmod(s, PACK)
+            b1_cols[s] = keep.tile([P, 1], F32, name="b1_col", bufs=PAGE_BUFS)
+            nc.sync.dma_start(b1_cols[s][:], b1_rows[b, t])
+
         gain_cols = keep.tile([P, PASSES, PACK], F32)
         nc.sync.dma_start(gain_cols[:], gain.rearrange("(b p t) -> p b t", b=PASSES, t=PACK))
 
         wgs_rows = wgs.rearrange("(p t) j -> p t j", t=PACK)
-        wgs_first = keep.tile([P, 1, S], F32)
-        wgs_rest = keep.tile([P, PACK - 1, S], F32)
-        for q in range(4):
-            nc.sync.dma_start(wgs_first[32 * q : 32 * q + 32], wgs_rows[:, 0:1, :])
-        idx2 = load_list("idx2", offs2)
+        wgs_tiles = {}
+
+        def load_wgs(t):
+            wgs_tiles[t] = keep.tile([P, S], F32, name=f"wgs{t}")
+            for q in range(4):
+                nc.sync.dma_start(wgs_tiles[t][32 * q : 32 * q + 32, :], wgs_rows[:, t, :])
+
+        load_wgs(0)
 
         page_rows = page0.rearrange("(b p t) c -> b t p c", b=PASSES, t=PACK)
         d_rows = d.rearrange("(b p t) m -> b t p m", b=PASSES, t=PACK)
@@ -85,33 +114,50 @@ def tile_list_wine_lot_sequencing_kernel(
 
         def load_slice(s):
             b, t = divmod(s, PACK)
-            pages[s] = four.tile([P, T2], F32, name="page")
+            pages[s] = keep.tile([P, T2], F32, name="page", bufs=PAGE_BUFS)
             nc.sync.dma_start(pages[s][:], page_rows[b, t])
-            d_tiles[s] = four.tile([P, PAIRS], F32, name="d_tile")
+            if s > 0:
+                load_b1(s)
+
+        def load_d(s):
+            b, t = divmod(s, PACK)
+            d_tiles[s] = keep.tile([P, PAIRS], F32, name="d_tile", bufs=PAGE_BUFS)
             nc.sync.dma_start(d_tiles[s][:], d_rows[b, t])
 
         load_slice(0)
+        idx2 = load_list("idx2", offs2)
+        load_b1(0)
+        load_d(0)
         idx3 = load_list("idx3", offs3)
         idx4 = load_list("idx4", offs4)
-        for q in range(4):
-            nc.sync.dma_start(wgs_rest[32 * q : 32 * q + 32], wgs_rows[:, 1:PACK, :])
-        load_slice(1)
+        load_wgs(1)
+        load_wgs(2)
         load_w1(1)
-        load_slice(2)
+        load_slice(1)
+        load_d(1)
+        load_wgs(3)
+        load_w2(1)
+        for s in range(2, PAGE_BUFS):
+            load_slice(s)
+            load_d(s)
         w3_raw = keep.tile([P, PASSES, PACK, N], F32)
         nc.sync.dma_start(w3_raw[:], w3.rearrange("(b p t) n -> p b t n", b=PASSES, t=PACK))
-        load_slice(3)
 
         w2_codes = keep.tile([P, H], U16, align_bytes=64)
-        nc.scalar.copy(
-            w2_codes[:].rearrange("p (b t m) -> p b t m", b=PASSES, t=PACK),
-            w2_raw[:].rearrange("p (b m t) -> p b t m", b=PASSES, t=PACK),
-        )
         w2_sc = keep.tile([P, H], U8, align_bytes=64)
-        nc.gpsimd.tensor_copy(
-            w2_sc[:].rearrange("p (b t m) -> p b t m", b=PASSES, t=PACK),
-            w2_raw_scales[:].rearrange("p (b m t) -> p b t m", b=PASSES, t=PACK),
-        )
+        for b in range(PASSES):
+            cols = slice(b * P * PACK, (b + 1) * P * PACK)
+            nc.scalar.copy(
+                w2_codes[:, cols].rearrange("p (t m) -> p t m", t=PACK),
+                w2_raw[b][:].rearrange("p (m t) -> p t m", t=PACK),
+            )
+            nc.gpsimd.tensor_copy(
+                w2_sc[:, cols].rearrange("p (t m) -> p t m", t=PACK),
+                w2_raw_scales[:, cols].rearrange("p (m t) -> p t m", t=PACK),
+            )
+
+        identity = keep.tile([P, P], F32)
+        make_identity(nc, identity[:])
 
         v_words, v_scales = {}, {}
 
@@ -122,54 +168,60 @@ def tile_list_wine_lot_sequencing_kernel(
             v_words[u] = keep.tile([P, BANK], U32, name=f"v_words{u}", align_bytes=64)
             nc.vector.tensor_copy(v_words[u][:], table_words[:].indirect(part))
 
-        w1_codes, w1_sc = {}, {}
+        w1_grouped, w1_codes, w1_sc = {}, {}, {}
+
+        def round_w1(s):
+            b, t = divmod(s, PACK)
+            w1_grouped[s] = keep.tile([P, P, PACK], BF16, name="w1_grouped", align_bytes=64)
+            copy = nc.vector.tensor_copy if s < 3 else nc.scalar.copy
+            copy(w1_grouped[s][:], w1_raw[b][:].rearrange("p j (m t) -> p t m j", t=PACK)[:, t])
 
         def quantize_w1(s):
-            b, t = divmod(s, PACK)
-            grouped = two.tile([P, P, PACK], BF16, name="w1_grouped", align_bytes=64)
-            nc.scalar.copy(grouped[:], w1_raw[b][:].rearrange("p j (m t) -> p t m j", t=PACK)[:, t])
-            w1_codes[s] = keep.tile([P, P], U32, name=f"w1_codes{s}", align_bytes=64)
-            w1_sc[s] = keep.tile([P, P], U8, name=f"w1_sc{s}", align_bytes=64)
+            w1_codes[s] = keep.tile([P, P], U32, name="w1_codes", align_bytes=64)
+            w1_sc[s] = keep.tile([P, P], U8, name="w1_sc", align_bytes=64)
             nc.vector.quantize_mx(
-                out=w1_codes[s][:].bitcast(FP8X4), scales=w1_sc[s][:], in_=grouped[:].rearrange("p m j -> p (m j)")
+                out=w1_codes[s][:].bitcast(FP8X4), scales=w1_sc[s][:], in_=w1_grouped[s][:].rearrange("p m j -> p (m j)")
             )
 
         factor, y1_banks, y2_tiles, h_tiles = {}, {}, {}, {}
 
         def products(s):
             b, t = divmod(s, PACK)
-            factor[s] = two.tile([P, S], F32, name="factor")
-            src = wgs_first[:, 0, :] if t == 0 else wgs_rest[:, t - 1, :]
-            nc.scalar.activation(factor[s][:], src, ACT.Copy, scale=gain_cols[:, b, t : t + 1])
-            y2_tiles[s] = three.tile([P, S], F32, name="y2")
+            factor[s] = two.tile([P, S], F32, name="factor", align_bytes=64)
+            src = wgs_tiles[t][:]
+            if s == 0:
+                nc.vector.tensor_scalar_mul(factor[s][:], src, gain_cols[:, b, t : t + 1])
+            else:
+                nc.scalar.activation(factor[s][:], src, ACT.Copy, scale=gain_cols[:, b, t : t + 1])
+            y2_tiles[s] = two.tile([P, S], F32, name="y2")
             cols = slice(s * P, (s + 1) * P)
             for u in range(HALVES):
-                y2_bank = psum.tile([P, BANK], F32, name="bank")
+                y2_bank = new_bank("y2")
                 nc.tensor.matmul_mx(
                     out=y2_bank[:], lhsT=w2_codes[:, cols].bitcast(FP4X4), lhsT_scale=w2_sc[:, cols],
                     rhs=v_words[u][:].bitcast(FP8X4), rhs_scale=v_scales[u][:], start=True, stop=True,
                 )
-                y1_banks[s, u] = psum.tile([P, BANK], F32, name="bank")
+                nc.scalar.copy(y2_tiles[s][:, u * BANK : (u + 1) * BANK], y2_bank[:])
+
+        def first_reading(s):
+            for u in range(HALVES):
+                y1_banks[s, u] = new_bank("y1")
                 nc.tensor.matmul_mx(
                     out=y1_banks[s, u][:], lhsT=w1_codes[s][:].bitcast(FP8X4), lhsT_scale=w1_sc[s][:],
                     rhs=v_words[u][:].bitcast(FP8X4), rhs_scale=v_scales[u][:], start=True, stop=True,
                 )
-                nc.scalar.copy(y2_tiles[s][:, u * BANK : (u + 1) * BANK], y2_bank[:])
 
         def lower_reading(s, u):
-            b, t = divmod(s, PACK)
             if u == 0:
-                h_tiles[s] = two.tile([P, S], F32, name="h")
+                h_tiles[s] = two.tile([P, S], F32, name="h", align_bytes=64)
             cols = slice(u * BANK, (u + 1) * BANK)
             nc.vector.scalar_tensor_tensor(
-                out=h_tiles[s][:, cols], in0=y1_banks[s, u][:], scalar=b1_cols[:, b, t : t + 1],
+                out=h_tiles[s][:, cols], in0=y1_banks[s, u][:], scalar=b1_cols[s][:],
                 in1=y2_tiles[s][:, cols], op0=ALU.add, op1=ALU.min,
             )
 
-        def put_h(s, first, last):
-            cols = slice(first * BANK, last * BANK)
-            part = idx2[:, first * (BANK // 16) : last * (BANK // 16)]
-            nc.vector.tensor_tensor(pages[s][:].indirect(part), h_tiles[s][:, cols], factor[s][:, cols], ALU.mult)
+        def put_h(s):
+            nc.vector.tensor_tensor(pages[s][:].indirect(idx2[:]), h_tiles[s][:], factor[s][:], ALU.mult)
 
         firsts, seconds = {}, {}
 
@@ -179,7 +231,25 @@ def tile_list_wine_lot_sequencing_kernel(
             seconds[s] = two.tile([P, PAIRS], F32, name="seconds")
             nc.vector.tensor_copy(seconds[s][:], pages[s][:].indirect(idx4[:]))
 
-        grouped_page, page_codes, page_sc, last_two = {}, {}, {}, {}
+        turned = {}
+
+        def turn_and_add(s):
+            bank = new_bank("turn")
+            for k in range(PAIRS // P):
+                cols = slice(k * P, (k + 1) * P)
+                nc.tensor.matmul(bank[:, cols], lhsT=firsts[s][:, cols], rhs=identity[:], is_transpose=True, start=True, stop=False)
+                nc.tensor.matmul(bank[:, cols], lhsT=d_tiles[s][:, cols], rhs=identity[:], is_transpose=True, start=False, stop=True)
+            turned[s] = two.tile([P, PAIRS], F32, name="turned")
+            nc.scalar.copy(turned[s][:], bank[:])
+
+        def turn_back(s, dst):
+            bank = new_bank("turn")
+            for k in range(PAIRS // P):
+                cols = slice(k * P, (k + 1) * P)
+                nc.tensor.transpose(bank[:, cols], turned[s][:, cols], identity[:])
+            nc.scalar.copy(dst, bank[:])
+
+        grouped_page, page_codes, page_sc, last_two, code_pairs = {}, {}, {}, {}, {}
 
         def round_slice(s, c, copy):
             b, t = divmod(s, PACK)
@@ -188,96 +258,125 @@ def tile_list_wine_lot_sequencing_kernel(
             copy(grouped_page[b, c][:, :, t], pages[s][:, c * BANK : (c + 1) * BANK])
 
         def quantize_page(b, c):
-            page_codes[b, c] = keep.tile([P, BANK], U32, name=f"page_codes{b}{c}", align_bytes=64)
+            if b == 0:
+                if c % 2 == 0:
+                    code_pairs[c // 2] = two.tile([P, 2, BANK], U32, name="code_pair", tag="h", align_bytes=64)
+                page_codes[b, c] = code_pairs[c // 2][:, c % 2, :]
+            else:
+                page_codes[b, c] = keep.tile([P, BANK], U32, name=f"page_codes{c}", align_bytes=64)
             page_sc[b, c] = keep.tile([P, BANK], U8, name=f"page_sc{b}{c}", align_bytes=64)
             nc.vector.quantize_mx(
                 out=page_codes[b, c][:].bitcast(FP8X4), scales=page_sc[b, c][:],
                 in_=grouped_page[b, c][:].rearrange("p m t -> p (m t)"),
             )
 
-        w3_codes = keep.tile([P, PASSES, N], U32, align_bytes=64)
-        w3_sc = keep.tile([P, PASSES, N], U8, align_bytes=64)
+        w3_grouped, w3_codes, w3_sc = {}, {}, {}
+
+        def round_w3(b):
+            w3_grouped[b] = two.tile([P, N, PACK], BF16, name="w3_grouped", align_bytes=64)
+            nc.scalar.copy(w3_grouped[b][:], w3_raw[:, b].rearrange("p t n -> p n t"))
 
         def quantize_w3(b):
-            grouped = two.tile([P, N, PACK], BF16, name="w3_grouped", align_bytes=64)
-            nc.scalar.copy(grouped[:], w3_raw[:, b].rearrange("p t n -> p n t"))
+            w3_codes[b] = two.tile([P, N], U32, name="w3_codes", tag="factor", align_bytes=64)
+            w3_sc[b] = two.tile([P, N], U8, name="w3_sc", align_bytes=64)
             nc.vector.quantize_mx(
-                out=w3_codes[:, b, :].bitcast(FP8X4), scales=w3_sc[:, b, :], in_=grouped[:].rearrange("p n t -> p (n t)")
+                out=w3_codes[b][:].bitcast(FP8X4), scales=w3_sc[b][:], in_=w3_grouped[b][:].rearrange("p n t -> p (n t)")
             )
 
         gather_table(0)
+        round_w1(0)
         quantize_w1(0)
         gather_table(1)
+        first_reading(0)
         products(0)
+        round_w1(1)
         quantize_w1(1)
         products(1)
         for u in range(HALVES):
             lower_reading(0, u)
-            put_h(0, u, u + 1)
-        for s in range(2, SLICES):
-            quantize_w1(s)
+        put_h(0)
+        first_reading(1)
+        round_w1(2)
+        quantize_w1(2)
+
+        def round_finished(s):
+            for c in range(CHUNKS):
+                if s + 2 < SLICES:
+                    round_slice(s, c, nc.scalar.copy)
+                else:
+                    last_two[c] = keep.tile([P, 2, BANK], BF16, name=f"last_two{c}")
+                    nc.scalar.copy(last_two[c][:, 0, :], pages[s][:, c * BANK : (c + 1) * BANK])
 
         for s in range(SLICES):
-            if s + 2 < SLICES:
-                products(s + 2)
             if s + 1 < SLICES:
                 for u in range(HALVES):
                     lower_reading(s + 1, u)
                 work = y2_tiles[s + 1]
             else:
-                work = three.tile([P, S], F32, name="y2")
+                work = two.tile([P, S], F32, name="y2")
             if s == 0:
                 fetch_pairs(0)
-            first_plus_d, larger = work[:, 0:PAIRS], work[:, PAIRS : 2 * PAIRS]
-            nc.vector.tensor_tensor(first_plus_d, firsts[s][:], d_tiles[s][:], ALU.add)
+            larger, first_plus_d = work[:, 0:PAIRS], work[:, PAIRS : 2 * PAIRS]
+            if s + 1 == SLICES:
+                larger = y2_tiles[s][:, PAIRS : 2 * PAIRS]
             nc.vector.tensor_tensor(larger, firsts[s][:], seconds[s][:], ALU.max)
+            if s > 0:
+                turn_back(s, first_plus_d)
+            else:
+                nc.vector.tensor_tensor(first_plus_d, firsts[s][:], d_tiles[s][:], ALU.add)
+            if s > 0:
+                round_finished(s - 1)
+                if s - 1 + PAGE_BUFS < SLICES:
+                    load_slice(s - 1 + PAGE_BUFS)
+                    load_d(s - 1 + PAGE_BUFS)
             if s + 1 < SLICES:
-                put_h(s + 1, 0, HALVES)
-            nc.vector.tensor_tensor(pages[s][:].indirect(idx3[:]), first_plus_d, seconds[s][:], ALU.add)
+                put_h(s + 1)
+            if s + 2 < SLICES:
+                first_reading(s + 2)
+            if s + 3 < SLICES:
+                round_w1(s + 3)
+            if 0 <= s - PACK < PASSES:
+                round_w3(s - PACK)
+            if s + 2 < SLICES:
+                products(s + 2)
+            nc.vector.tensor_copy(pages[s][:].indirect(idx4[:]), larger)
             if s + 1 < SLICES:
                 fetch_pairs(s + 1)
-            nc.vector.tensor_copy(pages[s][:].indirect(idx4[:]), larger)
-            if s + 2 < SLICES:
-                for c in range(CHUNKS):
-                    round_slice(s, c, nc.scalar.copy)
+                turn_and_add(s + 1)
+            nc.vector.tensor_tensor(pages[s][:].indirect(idx3[:]), first_plus_d, seconds[s][:], ALU.add)
+            if s + 3 < SLICES:
+                quantize_w1(s + 3)
             if s + 2 == SLICES:
-                for c in range(CHUNKS):
-                    last_two[c] = keep.tile([P, 2, BANK], BF16, name=f"last_two{c}")
-                    nc.scalar.copy(last_two[c][:, 0, :], pages[s][:, c * BANK : (c + 1) * BANK])
-            if s < PASSES:
-                quantize_w3(s)
-            if s == PACK - 1:
+                for b in range(PASSES):
+                    quantize_w3(b)
                 for c in range(CHUNKS):
                     quantize_page(0, c)
-            if s + 4 < SLICES:
-                load_slice(s + 4)
 
         groups = [(c, n) for c in range(CHUNKS) for n in range(N_TILES)]
         acc = {}
+        bank_tags = [tag for tag in ("spare", "y2", "y1", "turn") for k in range(bank_bufs[tag])]
+        results = [keep.tile([P, PACK, BANK], F32, name="results", tag=tag) for tag in ("w1_raw0", "w1_raw1", "w3_raw")]
 
         def second_stage_pass(c, n, b):
             if b == 0:
-                acc[c, n] = psum.tile([P, BANK], F32, name="bank")
+                acc[c, n] = new_bank(bank_tags[groups.index((c, n)) % BANKS])
             cols = slice(n * P, (n + 1) * P)
             nc.tensor.matmul_mx(
-                out=acc[c, n][:], lhsT=w3_codes[:, b, cols].bitcast(FP8X4), lhsT_scale=w3_sc[:, b, cols],
+                out=acc[c, n][:], lhsT=w3_codes[b][:, cols].bitcast(FP8X4), lhsT_scale=w3_sc[b][:, cols],
                 rhs=page_codes[b, c][:].bitcast(FP8X4), rhs_scale=page_sc[b, c][:], start=(b == 0), stop=(b == PASSES - 1),
             )
 
         for c, n in groups[:BANKS]:
             second_stage_pass(c, n, 0)
-        for step in range(CHUNKS + 2):
-            if step < CHUNKS:
-                nc.vector.tensor_copy(last_two[step][:, 1, :], pages[SLICES - 1][:, step * BANK : (step + 1) * BANK])
-            if 0 <= step - 1 < CHUNKS:
-                c = step - 1
-                nc.vector.tensor_copy(grouped_page[1, c][:, :, 2:PACK], last_two[c][:].rearrange("p e m -> p m e"))
-            if 0 <= step - 2:
-                quantize_page(1, step - 2)
+        for c in range(CHUNKS):
+            copy = nc.vector.tensor_copy if c == 0 else nc.scalar.copy
+            copy(last_two[c][:, 1, :], pages[SLICES - 1][:, c * BANK : (c + 1) * BANK])
+            nc.vector.tensor_copy(grouped_page[1, c][:, :, 2:PACK], last_two[c][:].rearrange("p e m -> p m e"))
+            quantize_page(1, c)
         for g, (c, n) in enumerate(groups):
             if g >= BANKS:
                 second_stage_pass(c, n, 0)
             second_stage_pass(c, n, 1)
-            result = four.tile([P, BANK], F32, name="result")
-            nc.scalar.activation(result[:], acc[c, n][:], ACT.Gelu_apprx_tanh)
-            nc.sync.dma_start(out[n * P : (n + 1) * P, c * BANK : (c + 1) * BANK], result[:])
+            result = results[g // PACK][:, g % PACK, :]
+            nc.scalar.activation(result, acc[c, n][:], ACT.Gelu_apprx_tanh)
+            nc.sync.dma_start(out[n * P : (n + 1) * P, c * BANK : (c + 1) * BANK], result)

@@ -27,6 +27,7 @@ CHUNKS = T2 // BANK
 N_TILES = N // P
 BANKS = 8
 PAGE_BUFS = 5
+EARLY_CHUNKS = 2
 
 
 def tile_list_wine_lot_sequencing_kernel(
@@ -86,7 +87,7 @@ def tile_list_wine_lot_sequencing_kernel(
         nc.gpsimd.memset(w2_raw_scales[:].bitcast(I32), 0)
         for q in range(4):
             rows = slice(32 * q, 32 * q + 4)
-            nc.gpsimd.tensor_copy(w2_raw_scales[rows, :].bitcast(I32), w2_rows[rows, :].bitcast(I32))
+            nc.scalar.copy(w2_raw_scales[rows, :].bitcast(U32), w2_rows[rows, :].bitcast(U32))
         b1_rows = b1.rearrange("(b p t o) -> b t p o", b=PASSES, t=PACK, o=1)
         b1_cols = {}
 
@@ -144,16 +145,20 @@ def tile_list_wine_lot_sequencing_kernel(
         nc.sync.dma_start(w3_raw[:], w3.rearrange("(b p t) n -> p b t n", b=PASSES, t=PACK))
 
         w2_codes = keep.tile([P, H], U16, align_bytes=64)
-        w2_sc = keep.tile([P, H], U8, align_bytes=64)
         for b in range(PASSES):
             cols = slice(b * P * PACK, (b + 1) * P * PACK)
             nc.scalar.copy(
                 w2_codes[:, cols].rearrange("p (t m) -> p t m", t=PACK),
                 w2_raw[b][:].rearrange("p (m t) -> p t m", t=PACK),
             )
-            nc.gpsimd.tensor_copy(
-                w2_sc[:, cols].rearrange("p (t m) -> p t m", t=PACK),
-                w2_raw_scales[:, cols].rearrange("p (m t) -> p t m", t=PACK),
+
+        w2_sc = {}
+
+        def deal_w2_scales(b):
+            w2_sc[b] = keep.tile([P, P * PACK], U8, name="w2_sc", tag=("w2_sc", "first_grouped")[b], align_bytes=64)
+            nc.vector.tensor_copy(
+                w2_sc[b][:].rearrange("p (t m) -> p t m", t=PACK),
+                w2_raw_scales[:, b * P * PACK : (b + 1) * P * PACK].rearrange("p (m t) -> p t m", t=PACK),
             )
 
         identity = keep.tile([P, P], F32)
@@ -172,7 +177,8 @@ def tile_list_wine_lot_sequencing_kernel(
 
         def round_w1(s):
             b, t = divmod(s, PACK)
-            w1_grouped[s] = keep.tile([P, P, PACK], BF16, name="w1_grouped", align_bytes=64)
+            tag = "first_grouped" if s == 0 else "w1_grouped"
+            w1_grouped[s] = keep.tile([P, P, PACK], BF16, name="w1_grouped", tag=tag, align_bytes=64)
             copy = nc.vector.tensor_copy if s < 3 else nc.scalar.copy
             copy(w1_grouped[s][:], w1_raw[b][:].rearrange("p j (m t) -> p t m j", t=PACK)[:, t])
 
@@ -198,7 +204,7 @@ def tile_list_wine_lot_sequencing_kernel(
             for u in range(HALVES):
                 y2_bank = new_bank("y2")
                 nc.tensor.matmul_mx(
-                    out=y2_bank[:], lhsT=w2_codes[:, cols].bitcast(FP4X4), lhsT_scale=w2_sc[:, cols],
+                    out=y2_bank[:], lhsT=w2_codes[:, cols].bitcast(FP4X4), lhsT_scale=w2_sc[b][:, t * P : (t + 1) * P],
                     rhs=v_words[u][:].bitcast(FP8X4), rhs_scale=v_scales[u][:], start=True, stop=True,
                 )
                 nc.scalar.copy(y2_tiles[s][:, u * BANK : (u + 1) * BANK], y2_bank[:])
@@ -249,7 +255,7 @@ def tile_list_wine_lot_sequencing_kernel(
                 nc.tensor.transpose(bank[:, cols], turned[s][:, cols], identity[:])
             nc.scalar.copy(dst, bank[:])
 
-        grouped_page, page_codes, page_sc, last_two, code_pairs = {}, {}, {}, {}, {}
+        grouped_page, page_codes, page_sc, last_two = {}, {}, {}, {}
 
         def round_slice(s, c, copy):
             b, t = divmod(s, PACK)
@@ -258,12 +264,12 @@ def tile_list_wine_lot_sequencing_kernel(
             copy(grouped_page[b, c][:, :, t], pages[s][:, c * BANK : (c + 1) * BANK])
 
         def quantize_page(b, c):
-            if b == 0:
-                if c % 2 == 0:
-                    code_pairs[c // 2] = two.tile([P, 2, BANK], U32, name="code_pair", tag="h", align_bytes=64)
-                page_codes[b, c] = code_pairs[c // 2][:, c % 2, :]
-            else:
+            if b == 1:
                 page_codes[b, c] = keep.tile([P, BANK], U32, name=f"page_codes{c}", align_bytes=64)
+            elif c < EARLY_CHUNKS:
+                page_codes[b, c] = early_codes[:, c, :]
+            else:
+                page_codes[b, c] = keep.tile([P, BANK], U32, name="late_codes", tag=f"last_two{c - EARLY_CHUNKS}", align_bytes=64)
             page_sc[b, c] = keep.tile([P, BANK], U8, name=f"page_sc{b}{c}", align_bytes=64)
             nc.vector.quantize_mx(
                 out=page_codes[b, c][:].bitcast(FP8X4), scales=page_sc[b, c][:],
@@ -287,6 +293,8 @@ def tile_list_wine_lot_sequencing_kernel(
         round_w1(0)
         quantize_w1(0)
         gather_table(1)
+        for b in range(PASSES):
+            deal_w2_scales(b)
         first_reading(0)
         products(0)
         round_w1(1)
@@ -304,7 +312,7 @@ def tile_list_wine_lot_sequencing_kernel(
                 if s + 2 < SLICES:
                     round_slice(s, c, nc.scalar.copy)
                 else:
-                    last_two[c] = keep.tile([P, 2, BANK], BF16, name=f"last_two{c}")
+                    last_two[c] = keep.tile([P, 2, BANK], BF16, name=f"last_two{c}", align_bytes=64)
                     nc.scalar.copy(last_two[c][:, 0, :], pages[s][:, c * BANK : (c + 1) * BANK])
 
         for s in range(SLICES):
@@ -349,7 +357,8 @@ def tile_list_wine_lot_sequencing_kernel(
             if s + 2 == SLICES:
                 for b in range(PASSES):
                     quantize_w3(b)
-                for c in range(CHUNKS):
+                early_codes = two.tile([P, EARLY_CHUNKS, BANK], U32, name="early_codes", tag="h", align_bytes=64)
+                for c in range(EARLY_CHUNKS):
                     quantize_page(0, c)
 
         groups = [(c, n) for c in range(CHUNKS) for n in range(N_TILES)]
@@ -366,15 +375,17 @@ def tile_list_wine_lot_sequencing_kernel(
                 rhs=page_codes[b, c][:].bitcast(FP8X4), rhs_scale=page_sc[b, c][:], start=(b == 0), stop=(b == PASSES - 1),
             )
 
-        for c, n in groups[:BANKS]:
+        for c, n in groups[: EARLY_CHUNKS * N_TILES]:
             second_stage_pass(c, n, 0)
         for c in range(CHUNKS):
             copy = nc.vector.tensor_copy if c == 0 else nc.scalar.copy
             copy(last_two[c][:, 1, :], pages[SLICES - 1][:, c * BANK : (c + 1) * BANK])
             nc.vector.tensor_copy(grouped_page[1, c][:, :, 2:PACK], last_two[c][:].rearrange("p e m -> p m e"))
+            if c >= EARLY_CHUNKS:
+                quantize_page(0, c)
             quantize_page(1, c)
         for g, (c, n) in enumerate(groups):
-            if g >= BANKS:
+            if c >= EARLY_CHUNKS:
                 second_stage_pass(c, n, 0)
             second_stage_pass(c, n, 1)
             result = results[g // PACK][:, g % PACK, :]

from contextlib import ExitStack

import concourse.mybir as mybir
from concourse.masks import make_identity

K, T, S, T2, PAIRS, H, N = 512, 2048, 1024, 2048, 512, 1024, 384
FLOPS = 2 * 2 * K * H * S + 2 * H * N * T2

F32 = mybir.dt.float32
BF16 = mybir.dt.bfloat16
I32 = mybir.dt.int32
U32 = mybir.dt.uint32
U16 = mybir.dt.uint16
U8 = mybir.dt.uint8
FP8X4 = mybir.dt.float8_e4m3fn_x4
FP4X4 = mybir.dt.float4_e2m1fn_x4
ALU = mybir.AluOpType
ACT = mybir.ActivationFunctionType

P = 128
PACK = 4
BANK = 512
PASSES = H // (P * PACK)
SLICES = PASSES * PACK
HALVES = S // BANK
CHUNKS = T2 // BANK
N_TILES = N // P
BANKS = 8
PAGE_BUFS = 5
EARLY_CHUNKS = 2


def tile_list_wine_lot_sequencing_kernel(
    tc, tab_words, tab_scales, offs, w1, b1, w2_words, w2_scales, gain, wgs, page0, offs2, offs3, offs4, d, w3, out
):
    nc = tc.nc
    with ExitStack() as ctx:
        lists = ctx.enter_context(tc.tile_pool(name="lists", bufs=1))
        keep = ctx.enter_context(tc.tile_pool(name="keep", bufs=1))
        two = ctx.enter_context(tc.tile_pool(name="two", bufs=2))
        four = ctx.enter_context(tc.tile_pool(name="four", bufs=4))
        psum = ctx.enter_context(tc.psum_pool(name="psum", bufs=2))
        bank_bufs = {"y1": HALVES, "y2": HALVES, "turn": 2, "spare": 2}

        def new_bank(tag):
            return psum.tile([P, BANK], F32, name="bank", tag=tag, bufs=bank_bufs[tag])


        def load_list(name, src):
            tile = lists.tile(list(src.shape), U16, name=name)
            nc.sync.dma_start(tile[:], src)
            return tile

        def load_scale_rows(queue, tile, src):
            for q in range(4):
                queue.dma_start(tile[32 * q : 32 * q + 4, :].bitcast(I32), src[0, 4 * q : 4 * q + 4, :].bitcast(I32))

        idx = load_list("idx", offs)
        table_rows = keep.tile([P, T], U8)
        load_scale_rows(nc.sync, table_rows, tab_scales)
        table_scales = keep.tile([P, T], U8, align_bytes=64)
        nc.vector.memset(table_scales[:].bitcast(I32), 0)
        for q in range(4):
            rows = slice(32 * q, 32 * q + 4)
            nc.vector.tensor_copy(table_scales[rows, :].bitcast(I32), table_rows[rows, :].bitcast(I32))
        table_words = keep.tile([P, T], U32, align_bytes=64)
        nc.sync.dma_start(table_words[:].bitcast(I32), tab_words[0].rearrange("p t i -> p (t i)").bitcast(I32))

        w1_rows = w1.rearrange("(p j) (b c) -> b p j c", j=PACK, b=PASSES)
        w1_raw = {}

        def load_w1(b):
            w1_raw[b] = keep.tile([P, PACK, P * PACK], F32, name=f"w1_raw{b}")
            nc.sync.dma_start(w1_raw[b][:], w1_rows[b])

        w2_rows = keep.tile([P, H], U8)
        load_scale_rows(nc.sync, w2_rows, w2_scales)
        w2_raw = {}

        def load_w2(b):
            w2_raw[b] = keep.tile([P, P * PACK], U16, name=f"w2_raw{b}")
            nc.sync.dma_start(w2_raw[b][:].bitcast(I32), w2_words[0, :, 2 * b * P * PACK : 2 * (b + 1) * P * PACK].bitcast(I32))

        load_w1(0)
        load_w2(0)
        w2_raw_scales = keep.tile([P, H], U8, align_bytes=64)
        nc.gpsimd.memset(w2_raw_scales[:].bitcast(I32), 0)
        for q in range(4):
            rows = slice(32 * q, 32 * q + 4)
            nc.scalar.copy(w2_raw_scales[rows, :].bitcast(U32), w2_rows[rows, :].bitcast(U32))
        b1_rows = b1.rearrange("(b p t o) -> b t p o", b=PASSES, t=PACK, o=1)
        b1_cols = {}

        def load_b1(s):
            b, t = divmod(s, PACK)
            b1_cols[s] = keep.tile([P, 1], F32, name="b1_col", bufs=PAGE_BUFS)
            nc.sync.dma_start(b1_cols[s][:], b1_rows[b, t])

        gain_cols = keep.tile([P, PASSES, PACK], F32)
        nc.sync.dma_start(gain_cols[:], gain.rearrange("(b p t) -> p b t", b=PASSES, t=PACK))

        wgs_rows = wgs.rearrange("(p t) j -> p t j", t=PACK)
        wgs_tiles = {}

        def load_wgs(t):
            wgs_tiles[t] = keep.tile([P, S], F32, name=f"wgs{t}")
            for q in range(4):
                nc.sync.dma_start(wgs_tiles[t][32 * q : 32 * q + 32, :], wgs_rows[:, t, :])

        load_wgs(0)

        page_rows = page0.rearrange("(b p t) c -> b t p c", b=PASSES, t=PACK)
        d_rows = d.rearrange("(b p t) m -> b t p m", b=PASSES, t=PACK)
        pages, d_tiles = {}, {}

        def load_slice(s):
            b, t = divmod(s, PACK)
            pages[s] = keep.tile([P, T2], F32, name="page", bufs=PAGE_BUFS)
            nc.sync.dma_start(pages[s][:], page_rows[b, t])
            if s > 0:
                load_b1(s)

        def load_d(s):
            b, t = divmod(s, PACK)
            d_tiles[s] = keep.tile([P, PAIRS], F32, name="d_tile", bufs=PAGE_BUFS)
            nc.sync.dma_start(d_tiles[s][:], d_rows[b, t])

        load_slice(0)
        idx2 = load_list("idx2", offs2)
        load_b1(0)
        load_d(0)
        idx3 = load_list("idx3", offs3)
        idx4 = load_list("idx4", offs4)
        load_wgs(1)
        load_wgs(2)
        load_w1(1)
        load_slice(1)
        load_d(1)
        load_wgs(3)
        load_w2(1)
        for s in range(2, PAGE_BUFS):
            load_slice(s)
            load_d(s)
        w3_raw = keep.tile([P, PASSES, PACK, N], F32)
        nc.sync.dma_start(w3_raw[:], w3.rearrange("(b p t) n -> p b t n", b=PASSES, t=PACK))

        w2_codes = keep.tile([P, H], U16, align_bytes=64)
        for b in range(PASSES):
            cols = slice(b * P * PACK, (b + 1) * P * PACK)
            nc.scalar.copy(
                w2_codes[:, cols].rearrange("p (t m) -> p t m", t=PACK),
                w2_raw[b][:].rearrange("p (m t) -> p t m", t=PACK),
            )

        w2_sc = {}

        def deal_w2_scales(b):
            w2_sc[b] = keep.tile([P, P * PACK], U8, name="w2_sc", tag=("w2_sc", "first_grouped")[b], align_bytes=64)
            nc.vector.tensor_copy(
                w2_sc[b][:].rearrange("p (t m) -> p t m", t=PACK),
                w2_raw_scales[:, b * P * PACK : (b + 1) * P * PACK].rearrange("p (m t) -> p t m", t=PACK),
            )

        identity = keep.tile([P, P], F32)
        make_identity(nc, identity[:])

        v_words, v_scales = {}, {}

        def gather_table(u):
            part = idx[:, u * (BANK // 16) : (u + 1) * (BANK // 16)]
            v_scales[u] = keep.tile([P, BANK], U8, name=f"v_scales{u}", align_bytes=64)
            nc.vector.tensor_copy(v_scales[u][:], table_scales[:].indirect(part))
            v_words[u] = keep.tile([P, BANK], U32, name=f"v_words{u}", align_bytes=64)
            nc.vector.tensor_copy(v_words[u][:], table_words[:].indirect(part))

        w1_grouped, w1_codes, w1_sc = {}, {}, {}

        def round_w1(s):
            b, t = divmod(s, PACK)
            tag = "first_grouped" if s == 0 else "w1_grouped"
            w1_grouped[s] = keep.tile([P, P, PACK], BF16, name="w1_grouped", tag=tag, align_bytes=64)
            copy = nc.vector.tensor_copy if s < 3 else nc.scalar.copy
            copy(w1_grouped[s][:], w1_raw[b][:].rearrange("p j (m t) -> p t m j", t=PACK)[:, t])

        def quantize_w1(s):
            w1_codes[s] = keep.tile([P, P], U32, name="w1_codes", align_bytes=64)
            w1_sc[s] = keep.tile([P, P], U8, name="w1_sc", align_bytes=64)
            nc.vector.quantize_mx(
                out=w1_codes[s][:].bitcast(FP8X4), scales=w1_sc[s][:], in_=w1_grouped[s][:].rearrange("p m j -> p (m j)")
            )

        factor, y1_banks, y2_tiles, h_tiles = {}, {}, {}, {}

        def products(s):
            b, t = divmod(s, PACK)
            factor[s] = two.tile([P, S], F32, name="factor", align_bytes=64)
            src = wgs_tiles[t][:]
            if s == 0:
                nc.vector.tensor_scalar_mul(factor[s][:], src, gain_cols[:, b, t : t + 1])
            else:
                nc.scalar.activation(factor[s][:], src, ACT.Copy, scale=gain_cols[:, b, t : t + 1])
            y2_tiles[s] = two.tile([P, S], F32, name="y2")
            cols = slice(s * P, (s + 1) * P)
            for u in range(HALVES):
                y2_bank = new_bank("y2")
                nc.tensor.matmul_mx(
                    out=y2_bank[:], lhsT=w2_codes[:, cols].bitcast(FP4X4), lhsT_scale=w2_sc[b][:, t * P : (t + 1) * P],
                    rhs=v_words[u][:].bitcast(FP8X4), rhs_scale=v_scales[u][:], start=True, stop=True,
                )
                nc.scalar.copy(y2_tiles[s][:, u * BANK : (u + 1) * BANK], y2_bank[:])

        def first_reading(s):
            for u in range(HALVES):
                y1_banks[s, u] = new_bank("y1")
                nc.tensor.matmul_mx(
                    out=y1_banks[s, u][:], lhsT=w1_codes[s][:].bitcast(FP8X4), lhsT_scale=w1_sc[s][:],
                    rhs=v_words[u][:].bitcast(FP8X4), rhs_scale=v_scales[u][:], start=True, stop=True,
                )

        def lower_reading(s, u):
            if u == 0:
                h_tiles[s] = two.tile([P, S], F32, name="h", align_bytes=64)
            cols = slice(u * BANK, (u + 1) * BANK)
            nc.vector.scalar_tensor_tensor(
                out=h_tiles[s][:, cols], in0=y1_banks[s, u][:], scalar=b1_cols[s][:],
                in1=y2_tiles[s][:, cols], op0=ALU.add, op1=ALU.min,
            )

        def put_h(s):
            nc.vector.tensor_tensor(pages[s][:].indirect(idx2[:]), h_tiles[s][:], factor[s][:], ALU.mult)

        firsts, seconds = {}, {}

        def fetch_pairs(s):
            firsts[s] = two.tile([P, PAIRS], F32, name="firsts")
            nc.vector.tensor_copy(firsts[s][:], pages[s][:].indirect(idx3[:]))
            seconds[s] = two.tile([P, PAIRS], F32, name="seconds")
            nc.vector.tensor_copy(seconds[s][:], pages[s][:].indirect(idx4[:]))

        turned = {}

        def turn_and_add(s):
            bank = new_bank("turn")
            for k in range(PAIRS // P):
                cols = slice(k * P, (k + 1) * P)
                nc.tensor.matmul(bank[:, cols], lhsT=firsts[s][:, cols], rhs=identity[:], is_transpose=True, start=True, stop=False)
                nc.tensor.matmul(bank[:, cols], lhsT=d_tiles[s][:, cols], rhs=identity[:], is_transpose=True, start=False, stop=True)
            turned[s] = two.tile([P, PAIRS], F32, name="turned")
            nc.scalar.copy(turned[s][:], bank[:])

        def turn_back(s, dst):
            bank = new_bank("turn")
            for k in range(PAIRS // P):
                cols = slice(k * P, (k + 1) * P)
                nc.tensor.transpose(bank[:, cols], turned[s][:, cols], identity[:])
            nc.scalar.copy(dst, bank[:])

        grouped_page, page_codes, page_sc, last_two = {}, {}, {}, {}

        def round_slice(s, c, copy):
            b, t = divmod(s, PACK)
            if t == 0:
                grouped_page[b, c] = two.tile([P, BANK, PACK], BF16, name=f"grouped_page{c}", align_bytes=64)
            copy(grouped_page[b, c][:, :, t], pages[s][:, c * BANK : (c + 1) * BANK])

        def quantize_page(b, c):
            if b == 1:
                page_codes[b, c] = keep.tile([P, BANK], U32, name=f"page_codes{c}", align_bytes=64)
            elif c < EARLY_CHUNKS:
                page_codes[b, c] = early_codes[:, c, :]
            else:
                page_codes[b, c] = keep.tile([P, BANK], U32, name="late_codes", tag=f"last_two{c - EARLY_CHUNKS}", align_bytes=64)
            page_sc[b, c] = keep.tile([P, BANK], U8, name=f"page_sc{b}{c}", align_bytes=64)
            nc.vector.quantize_mx(
                out=page_codes[b, c][:].bitcast(FP8X4), scales=page_sc[b, c][:],
                in_=grouped_page[b, c][:].rearrange("p m t -> p (m t)"),
            )

        w3_grouped, w3_codes, w3_sc = {}, {}, {}

        def round_w3(b):
            w3_grouped[b] = two.tile([P, N, PACK], BF16, name="w3_grouped", align_bytes=64)
            nc.scalar.copy(w3_grouped[b][:], w3_raw[:, b].rearrange("p t n -> p n t"))

        def quantize_w3(b):
            w3_codes[b] = two.tile([P, N], U32, name="w3_codes", tag="factor", align_bytes=64)
            w3_sc[b] = two.tile([P, N], U8, name="w3_sc", align_bytes=64)
            nc.vector.quantize_mx(
                out=w3_codes[b][:].bitcast(FP8X4), scales=w3_sc[b][:], in_=w3_grouped[b][:].rearrange("p n t -> p (n t)")
            )

        gather_table(0)
        round_w1(0)
        quantize_w1(0)
        gather_table(1)
        for b in range(PASSES):
            deal_w2_scales(b)
        first_reading(0)
        products(0)
        round_w1(1)
        quantize_w1(1)
        products(1)
        for u in range(HALVES):
            lower_reading(0, u)
        put_h(0)
        first_reading(1)
        round_w1(2)
        quantize_w1(2)

        def round_finished(s):
            for c in range(CHUNKS):
                if s + 2 < SLICES:
                    round_slice(s, c, nc.scalar.copy)
                else:
                    last_two[c] = keep.tile([P, 2, BANK], BF16, name=f"last_two{c}", align_bytes=64)
                    nc.scalar.copy(last_two[c][:, 0, :], pages[s][:, c * BANK : (c + 1) * BANK])

        for s in range(SLICES):
            if s + 1 < SLICES:
                for u in range(HALVES):
                    lower_reading(s + 1, u)
                work = y2_tiles[s + 1]
            else:
                work = two.tile([P, S], F32, name="y2")
            if s == 0:
                fetch_pairs(0)
            larger, first_plus_d = work[:, 0:PAIRS], work[:, PAIRS : 2 * PAIRS]
            if s + 1 == SLICES:
                larger = y2_tiles[s][:, PAIRS : 2 * PAIRS]
            nc.vector.tensor_tensor(larger, firsts[s][:], seconds[s][:], ALU.max)
            if s > 0:
                turn_back(s, first_plus_d)
            else:
                nc.vector.tensor_tensor(first_plus_d, firsts[s][:], d_tiles[s][:], ALU.add)
            if s > 0:
                round_finished(s - 1)
                if s - 1 + PAGE_BUFS < SLICES:
                    load_slice(s - 1 + PAGE_BUFS)
                    load_d(s - 1 + PAGE_BUFS)
            if s + 1 < SLICES:
                put_h(s + 1)
            if s + 2 < SLICES:
                first_reading(s + 2)
            if s + 3 < SLICES:
                round_w1(s + 3)
            if 0 <= s - PACK < PASSES:
                round_w3(s - PACK)
            if s + 2 < SLICES:
                products(s + 2)
            nc.vector.tensor_copy(pages[s][:].indirect(idx4[:]), larger)
            if s + 1 < SLICES:
                fetch_pairs(s + 1)
                turn_and_add(s + 1)
            nc.vector.tensor_tensor(pages[s][:].indirect(idx3[:]), first_plus_d, seconds[s][:], ALU.add)
            if s + 3 < SLICES:
                quantize_w1(s + 3)
            if s + 2 == SLICES:
                for b in range(PASSES):
                    quantize_w3(b)
                early_codes = two.tile([P, EARLY_CHUNKS, BANK], U32, name="early_codes", tag="h", align_bytes=64)
                for c in range(EARLY_CHUNKS):
                    quantize_page(0, c)

        groups = [(c, n) for c in range(CHUNKS) for n in range(N_TILES)]
        acc = {}
        bank_tags = [tag for tag in ("spare", "y2", "y1", "turn") for k in range(bank_bufs[tag])]
        results = [keep.tile([P, PACK, BANK], F32, name="results", tag=tag) for tag in ("w1_raw0", "w1_raw1", "w3_raw")]

        def second_stage_pass(c, n, b):
            if b == 0:
                acc[c, n] = new_bank(bank_tags[groups.index((c, n)) % BANKS])
            cols = slice(n * P, (n + 1) * P)
            nc.tensor.matmul_mx(
                out=acc[c, n][:], lhsT=w3_codes[b][:, cols].bitcast(FP8X4), lhsT_scale=w3_sc[b][:, cols],
                rhs=page_codes[b, c][:].bitcast(FP8X4), rhs_scale=page_sc[b, c][:], start=(b == 0), stop=(b == PASSES - 1),
            )

        for c, n in groups[: EARLY_CHUNKS * N_TILES]:
            second_stage_pass(c, n, 0)
        for c in range(CHUNKS):
            copy = nc.vector.tensor_copy if c == 0 else nc.scalar.copy
            copy(last_two[c][:, 1, :], pages[SLICES - 1][:, c * BANK : (c + 1) * BANK])
            nc.vector.tensor_copy(grouped_page[1, c][:, :, 2:PACK], last_two[c][:].rearrange("p e m -> p m e"))
            if c >= EARLY_CHUNKS:
                quantize_page(0, c)
            quantize_page(1, c)
        for g, (c, n) in enumerate(groups):
            if c >= EARLY_CHUNKS:
                second_stage_pass(c, n, 0)
            second_stage_pass(c, n, 1)
            result = results[g // PACK][:, g % PACK, :]
            nc.scalar.activation(result, acc[c, n][:], ACT.Gelu_apprx_tanh)
            nc.sync.dma_start(out[n * P : (n + 1) * P, c * BANK : (c + 1) * BANK], result)
